import numpy as np
import ml_dtypes


def mxq(x, axis, fmt="e4m3"):
    dtype, down = {"e4m3": (ml_dtypes.float8_e4m3fn, 7), "e5m2": (ml_dtypes.float8_e5m2, 14)}[fmt]
    v = np.moveaxis(np.asarray(x, np.float32).astype(ml_dtypes.bfloat16).astype(np.float64), axis, -1)
    blocks = v.reshape(v.shape[:-1] + (-1, 32))
    amax = np.abs(blocks).max(-1, keepdims=True)
    byte = np.maximum(np.where(amax > 0, np.frexp(amax)[1] - 1 + 127, 0) - down, 1)
    scale = np.exp2(byte - 127.0)
    codes = (blocks / scale).astype(np.float32).astype(dtype).astype(np.float64)
    return np.moveaxis((codes * scale).reshape(v.shape), -1, axis)


WIDE = False


def mx_kscale(k):
    if not WIDE:
        return np.ones(k)
    levels = np.array([10, -10, 5, -5, 0])
    if k % 512:
        return np.exp2(np.random.permutation(np.resize(levels, k // 32))).repeat(32)
    a = np.empty((k // 512, 16))
    for p in range(k // 512):
        a[p, :8] = np.random.permutation(np.resize(levels, 8))
        for g in range(8):
            far = levels[np.abs(levels - a[p, g]) >= 10]
            a[p, g + 8] = far[np.random.randint(len(far))]
    return np.exp2(a.ravel()).repeat(32)


def f64(x):
    return np.asarray(x).astype(np.float64)


def striped(idx):
    return np.tile(np.asarray(idx).reshape(-1, 16).T, (8, 1)).astype(np.uint16)


def unstriped(offs):
    return offs[:16].T.reshape(-1).astype(np.int64)


def striped8(idx):
    return np.asarray(idx).reshape(8, -1, 16).transpose(0, 2, 1).reshape(128, -1).astype(np.uint16)


def unstriped8(offs):
    return offs.reshape(8, 16, -1).transpose(0, 2, 1).reshape(8, -1).astype(np.int64)


def pick8(x, idx, run):
    r = np.arange(len(x))
    return x[r[:, None], idx[r % (8 * run) // run]]


E2M1 = np.array([0.0, 0.5, 1.0, 1.5, 2.0, 3.0, 4.0, 6.0, -0.0, -0.5, -1.0, -1.5, -2.0, -3.0, -4.0, -6.0])


def pack_weight(w, fmt):
    k, n = w.shape
    w = f64(np.asarray(w, np.float32).astype(ml_dtypes.bfloat16)).reshape(k // 32, 32, n)
    amax = np.abs(w).max(1)
    if fmt == "e4m3":
        byte = np.frexp(amax)[1] - 1 + 127 - 7
    else:
        mant, ex = np.frexp(amax / 6.0)
        byte = np.where(mant > 0.5, ex, ex - 1) + 127
    byte = np.clip(np.where(amax > 0, byte, 1), 1, 254)
    scaled = (w * np.exp2(127.0 - byte)[:, None, :]).reshape(k, n).astype(np.float32)
    by_word = np.ascontiguousarray(scaled.reshape(k // 512, 128, 4, n).transpose(0, 1, 3, 2))
    if fmt == "e4m3":
        words = by_word.astype(ml_dtypes.float8_e4m3fn).view(np.uint8)
    else:
        c = by_word.astype(ml_dtypes.float4_e2m1fn).view(np.uint8) & 0xF
        words = (c[..., 0::2] | (c[..., 1::2] << 4)).reshape(k // 512, 128, 2 * n)
    return np.ascontiguousarray(words), np.ascontiguousarray(byte.astype(np.uint8).reshape(k // 512, 16, n))


def unpack_weight(words, scales, fmt):
    g, _, n = scales.shape
    words = np.ascontiguousarray(words).reshape(g, 128, n, -1)
    if fmt == "e4m3":
        vals = words.view(ml_dtypes.float8_e4m3fn).astype(np.float64)
    else:
        nib = np.empty((g, 128, n, 4), np.uint8)
        nib[..., 0::2] = words & 0xF
        nib[..., 1::2] = words >> 4
        vals = E2M1[nib]
    vals = vals * np.repeat(np.exp2(scales.astype(np.float64) - 127.0), 8, axis=1)[..., None]
    return vals.transpose(0, 1, 3, 2).reshape(g * 512, n)


def sgn(shape):
    return np.random.uniform(0.5, 2.0, shape) * np.where(np.random.standard_normal(shape) < 0, -1.0, 1.0)


K, J, R, T, U, Z, M, O, D, N, E, G = 512, 512, 512, 1024, 1024, 512, 1024, 256, 1024, 256, 128, 512


def setup_inputs():
    n = np.random.standard_normal
    idx = np.stack([np.random.permutation(T)[:J] for _ in range(8)])
    idx2 = np.stack([np.random.permutation(U)[:J] for _ in range(8)])
    idx3 = np.random.permutation(M)[:J]
    idx4 = np.stack([np.random.permutation(J)[:O] for _ in range(8)])
    idx5 = np.stack([np.random.permutation(D)[:O] for _ in range(8)])
    idx6 = np.stack([np.random.permutation(O)[:E] for _ in range(8)])
    idx7 = np.stack([np.random.permutation(G)[:E] for _ in range(8)])
    fk = mx_kscale(K)
    fr = mx_kscale(R)
    fz = mx_kscale(Z)
    wp = pack_weight(n((K, R)) * 1 / np.sqrt(K) / fk[:, None] * fr, "e4m3")
    xop = pack_weight(n((Z, M)) / fz[:, None], "e4m3")
    w2p = pack_weight(n((Z, R)) * 1 / np.sqrt(Z) * fz[:, None] * fr, "e2m1")
    wbp = pack_weight(n((R, N)) * 1 / np.sqrt(R) / fr[:, None], "e2m1")
    return {
        "ta": (np.random.randint(-7, 8, (K, T)).astype(np.float64)).astype(np.float32),
        "tb": (np.random.randint(-7, 8, (K, U)).astype(np.float64)).astype(np.float32),
        "ga": ((np.random.randint(8, 25, (K, 1)) / 64.0) * fk[:, None]).astype(np.float32),
        "gb": ((np.random.randint(8, 25, (K, 1)) / 64.0) * fk[:, None]).astype(np.float32),
        "w_words": wp[0],
        "w_scales": wp[1],
        "xo_words": xop[0],
        "xo_scales": xop[1],
        "w2_words": w2p[0],
        "w2_scales": w2p[1],
        "tl": (np.random.randint(-7, 8, (R, D)).astype(np.float64)).astype(np.float32),
        "sa": (np.random.uniform(0.5, 1.6, (R, 1))).astype(np.float32),
        "sl": ((np.random.randint(6, 19, (R, 1)) / 64.0) * fr[:, None]).astype(np.float32),
        "wb_words": wbp[0],
        "wb_scales": wbp[1],
        "so": (sgn((N, 1))).astype(np.float32),
        "offs": striped8(idx),
        "offs2": striped8(idx2),
        "offs3": striped(idx3),
        "offs4": striped8(idx4),
        "offs5": striped8(idx5),
        "offs6": striped8(idx6),
        "offs7": striped8(idx7),
    }


def reference(ta, tb, ga, gb, w_words, w_scales, xo_words, xo_scales, w2_words, w2_scales, tl, sa, sl, wb_words, wb_scales, so, offs, offs2, offs3, offs4, offs5, offs6, offs7):
    idx = unstriped8(offs)
    idx2 = unstriped8(offs2)
    idx3 = unstriped(offs3)
    idx4 = unstriped8(offs4)
    idx5 = unstriped8(offs5)
    idx6 = unstriped8(offs6)
    idx7 = unstriped8(offs7)
    wu = unpack_weight(w_words, w_scales, "e4m3")
    xou = unpack_weight(xo_words, xo_scales, "e4m3")
    w2u = unpack_weight(w2_words, w2_scales, "e2m1")
    wbu = unpack_weight(wb_words, wb_scales, "e2m1")
    xc = np.maximum(pick8(f64(ta), idx, 64) * f64(ga), pick8(f64(tb), idx2, 64) * f64(gb))
    xcq = mxq(xc, 0, "e4m3")
    xoidx3g = xou[:, idx3]
    a = wu.T @ xcq + w2u.T @ xoidx3g
    hid = np.maximum(pick8(a, idx4, 64) * f64(sa), pick8(f64(tl), idx5, 64) * f64(sl))
    hidq = mxq(hid, 0, "e4m3")
    p = wbu.T @ hidq
    m0 = pick8(p, idx6, 16) * f64(so)
    y = np.zeros((N, G))
    y[np.arange(N)[:, None], idx7[np.arange(N) % 128 // 16]] = m0
    return y

@@ -1,0 +1,234 @@
+from contextlib import ExitStack
+
+import concourse.mybir as mybir
+
+F32 = mybir.dt.float32
+BF16 = mybir.dt.bfloat16
+I32 = mybir.dt.int32
+U32 = mybir.dt.uint32
+U16 = mybir.dt.uint16
+U8 = mybir.dt.uint8
+FP8X4 = mybir.dt.float8_e4m3fn_x4
+FP4X4 = mybir.dt.float4_e2m1fn_x4
+COPY = mybir.ActivationFunctionType.Copy
+MAX = mybir.AluOpType.max
+
+K, J, R, T, Z, M, O, D, N, E, G = 512, 512, 512, 1024, 512, 1024, 256, 1024, 256, 128, 512
+FLOPS = 2 * K * R * J + 2 * Z * R * J + 2 * R * N * O
+
+P = 128
+PACK = 4
+HALF = J // 2
+QUADS = 4
+
+
+def tile_picked_largercode_plain_bank_codedlevel_one_posted_kernel(
+    tc, ta, tb, ga, gb, w_words, w_scales, xo_words, xo_scales, w2_words, w2_scales, tl, sa, sl,
+    wb_words, wb_scales, so, offs, offs2, offs3, offs4, offs5, offs6, offs7, out,
+):
+    nc = tc.nc
+    with ExitStack() as ctx:
+        keep = ctx.enter_context(tc.tile_pool(name="keep", bufs=1))
+        psum = ctx.enter_context(tc.psum_pool(name="psum", bufs=1))
+
+        def sb(name, shape, dtype):
+            return keep.tile(shape, dtype, name=name, align_bytes=64)
+
+        def load_list(name, src):
+            lst = sb(name, list(src.shape), U16)
+            nc.sync.dma_start(lst[:], src)
+            return lst
+
+        def load_rows(name, src, t):
+            rows = sb(name, [P, src.shape[1]], F32)
+            nc.sync.dma_start(rows[:], src.rearrange("(p t) c -> p t c", t=PACK)[:, t, :])
+            return rows
+
+        def load_factor(name, src, queue):
+            fac = sb(name, [P, PACK], F32)
+            queue.dma_start(fac[:], src.rearrange("(p t) o -> p (t o)", t=PACK))
+            return fac
+
+        def load_words(name, src, dtype, cols):
+            words = sb(name, [P, cols], dtype)
+            nc.sync.dma_start(words[:].bitcast(I32), src.bitcast(I32))
+            return words
+
+        def stage_scales(stage, src, first):
+            rows = src[0].bitcast(I32).rearrange("(q r) c -> r q c", r=4)
+            nc.sync.dma_start(stage[:, :, first : first + rows.shape[2]], rows)
+
+        def spread_scales(plane, stage):
+            words = plane[:].bitcast(I32)
+            nc.vector.memset(words, 0)
+            for q in range(QUADS):
+                nc.vector.tensor_copy(words[32 * q : 32 * q + 4, :], stage[:, q, :])
+
+        ga_sb = load_factor("ga_sb", ga, nc.scalar)
+        gb_sb = load_factor("gb_sb", gb, nc.scalar)
+        sl_sb = load_factor("sl_sb", sl, nc.gpsimd)
+        sa_sb = load_factor("sa_sb", sa, nc.gpsimd)
+        so_sb = sb("so_sb", [P, N // P], F32)
+        with nc.allow_non_contiguous_dma(reason="one factor a partition for each output tile"):
+            nc.gpsimd.dma_start(so_sb[:], so.rearrange("(t p) o -> p (t o)", p=P))
+        xo_stage = sb("xo_stage", [4, QUADS, M // 4], I32)
+        w_stage = sb("w_stage", [4, QUADS, (R + R + N) // 4], I32)
+
+        ta_sb, tb_sb, tl_sb = [], [], []
+        ta_sb.append(load_rows("ta0", ta, 0))
+        l1 = load_list("l1", offs)
+        tb_sb.append(load_rows("tb0", tb, 0))
+        l2 = load_list("l2", offs2)
+        ta_sb.append(load_rows("ta1", ta, 1))
+        stage_scales(xo_stage, xo_scales, 0)
+        tb_sb.append(load_rows("tb1", tb, 1))
+        l3 = load_list("l3", offs3)
+        xo_sb = load_words("xo_sb", xo_words[0].rearrange("p n t -> p (n t)"), U32, M)
+        stage_scales(w_stage, w2_scales, R // 4)
+        ta_sb.append(load_rows("ta2", ta, 2))
+        stage_scales(w_stage, w_scales, 0)
+        w2_sb = load_words("w2_sb", w2_words[0], U8, 2 * R)
+        stage_scales(w_stage, wb_scales, 2 * R // 4)
+        tb_sb.append(load_rows("tb2", tb, 2))
+        w_sb = load_words("w_sb", w_words[0].rearrange("p n t -> p (n t)"), I32, R)
+        ta_sb.append(load_rows("ta3", ta, 3))
+        tb_sb.append(load_rows("tb3", tb, 3))
+        l5 = load_list("l5", offs5)
+        tl_sb.append(load_rows("tl0", tl, 0))
+        l4 = load_list("l4", offs4)
+        for t in range(1, PACK):
+            tl_sb.append(load_rows(f"tl{t}", tl, t))
+        wb_sb = load_words("wb_sb", wb_words[0], U8, 2 * N)
+        l6 = load_list("l6", offs6)
+        l7 = load_list("l7", offs7)
+
+        pages = [sb(f"page{t}", [P, G], F32) for t in range(N // P)]
+        for page in pages:
+            nc.vector.memset(page[:], 0.0)
+        xo_plane = sb("xo_plane", [P, M], U8)
+        spread_scales(xo_plane, xo_stage)
+        w_plane = sb("w_plane", [P, R + R + N], U8)
+        spread_scales(w_plane, w_stage)
+        dealt_plane = sb("dealt_plane", [P, 2, R], U8)
+        nc.vector.tensor_copy(
+            dealt_plane[:].rearrange("p a (t m) -> p a t m", t=PACK),
+            w_plane[:, : 2 * R].rearrange("p (a m t) -> p a t m", a=2, t=PACK),
+        )
+        xo_picked_scales = sb("xo_picked_scales", [P, J], U8)
+        nc.vector.tensor_copy(xo_picked_scales[:], xo_plane[:].indirect(l3[:]))
+
+        def fetch(dst, window, offsets, factor):
+            nc.scalar.activation(dst, window[:].indirect(offsets), COPY, scale=factor)
+
+        def larger_pair(dst, first, second, u):
+            nc.vector.tensor_tensor(
+                dst[:, :, 2 * u : 2 * u + 2],
+                first.rearrange("p t j -> p j t"),
+                second.rearrange("p t j -> p j t"),
+                MAX,
+            )
+
+        xc = [sb(f"xc{h}", [P, HALF, PACK], BF16) for h in range(2)]
+        low_a = sb("low_a", [P, 2, J], F32)
+        low_b = sb("low_b", [P, 2, J], F32)
+        for t in range(2):
+            fetch(low_a[:, t, :], ta_sb[t], l1[:], ga_sb[:, t : t + 1])
+            fetch(low_b[:, t, :], tb_sb[t], l2[:], gb_sb[:, t : t + 1])
+        for h in range(2):
+            cols = slice(h * HALF, (h + 1) * HALF)
+            larger_pair(xc[h], low_a[:, :, cols], low_b[:, :, cols], 0)
+
+        xo_picked = sb("xo_picked", [P, J], U32)
+        nc.vector.tensor_copy(xo_picked[:], xo_sb[:].indirect(l3[:]))
+        w2_dealt = sb("w2_dealt", [P, 2 * R], U8)
+        nc.vector.tensor_copy(
+            w2_dealt[:].rearrange("p (t m b) -> p t m b", t=PACK, b=2),
+            w2_sb[:].rearrange("p (m t b) -> p t m b", t=PACK, b=2),
+        )
+        w_dealt = sb("w_dealt", [P, R], I32)
+        nc.vector.tensor_copy(
+            w_dealt[:].rearrange("p (t m) -> p t m", t=PACK),
+            w_sb[:].rearrange("p (m t) -> p t m", t=PACK),
+        )
+        banks = [[psum.tile([P, HALF], F32, name=f"bank{h}{t}") for t in range(PACK)] for h in range(2)]
+        for h in range(2):
+            cols = slice(h * HALF, (h + 1) * HALF)
+            for t in range(PACK):
+                nc.tensor.matmul_mx(
+                    out=banks[h][t][:],
+                    lhsT=w2_dealt[:, 2 * P * t : 2 * P * (t + 1)].bitcast(FP4X4),
+                    lhsT_scale=dealt_plane[:, 1, P * t : P * (t + 1)],
+                    rhs=xo_picked[:, cols].bitcast(FP8X4),
+                    rhs_scale=xo_picked_scales[:, cols],
+                    start=True,
+                    stop=False,
+                )
+
+        high_a = [sb(f"high_a{h}", [P, 2, HALF], F32) for h in range(2)]
+        high_b = [sb(f"high_b{h}", [P, 2, HALF], F32) for h in range(2)]
+        for t in range(2, PACK):
+            for h in range(2):
+                entries = slice(h * HALF // 16, (h + 1) * HALF // 16)
+                fetch(high_a[h][:, t - 2, :], ta_sb[t], l1[:, entries], ga_sb[:, t : t + 1])
+                fetch(high_b[h][:, t - 2, :], tb_sb[t], l2[:, entries], gb_sb[:, t : t + 1])
+        xc_codes = [sb(f"xc_codes{h}", [P, HALF], U32) for h in range(2)]
+        xc_scales = [sb(f"xc_scales{h}", [P, HALF], U8) for h in range(2)]
+        for h in range(2):
+            larger_pair(xc[h], high_a[h][:], high_b[h][:], 1)
+        for h in range(2):
+            nc.vector.quantize_mx(
+                out=xc_codes[h][:].bitcast(FP8X4),
+                scales=xc_scales[h][:],
+                in_=xc[h][:].rearrange("p j t -> p (j t)"),
+            )
+            for t in range(PACK):
+                nc.tensor.matmul_mx(
+                    out=banks[h][t][:],
+                    lhsT=w_dealt[:, P * t : P * (t + 1)].bitcast(FP8X4),
+                    lhsT_scale=dealt_plane[:, 0, P * t : P * (t + 1)],
+                    rhs=xc_codes[h][:].bitcast(FP8X4),
+                    rhs_scale=xc_scales[h][:],
+                    start=False,
+                    stop=True,
+                )
+
+        a_sb = [sb(f"a{t}", [P, J], F32) for t in range(PACK)]
+        hid = sb("hid", [P, O, PACK], BF16)
+        hid_a = [sb(f"hid_a{u}", [P, 2, O], F32) for u in range(2)]
+        hid_l = [sb(f"hid_l{u}", [P, 2, O], F32) for u in range(2)]
+        for t in range(PACK):
+            for h in range(2):
+                nc.vector.tensor_copy(a_sb[t][:, h * HALF : (h + 1) * HALF], banks[h][t][:])
+        for t in range(PACK):
+            fetch(hid_a[t // 2][:, t % 2, :], a_sb[t], l4[:], sa_sb[:, t : t + 1])
+            fetch(hid_l[t // 2][:, t % 2, :], tl_sb[t], l5[:], sl_sb[:, t : t + 1])
+            if t % 2 == 1:
+                larger_pair(hid, hid_a[t // 2][:], hid_l[t // 2][:], t // 2)
+        hid_codes = sb("hid_codes", [P, O], U32)
+        hid_scales = sb("hid_scales", [P, O], U8)
+        nc.vector.quantize_mx(
+            out=hid_codes[:].bitcast(FP8X4),
+            scales=hid_scales[:],
+            in_=hid[:].rearrange("p o t -> p (o t)"),
+        )
+
+        for t in range(N // P):
+            bank = psum.tile([P, O], F32, name=f"bank0{t}")
+            nc.tensor.matmul_mx(
+                out=bank[:],
+                lhsT=wb_sb[:, 2 * P * t : 2 * P * (t + 1)].bitcast(FP4X4),
+                lhsT_scale=w_plane[:, 2 * R + P * t : 2 * R + P * (t + 1)],
+                rhs=hid_codes[:].bitcast(FP8X4),
+                rhs_scale=hid_scales[:],
+                start=True,
+                stop=True,
+            )
+            p_sb = sb(f"p{t}", [P, O], F32)
+            if t == 0:
+                nc.scalar.copy(p_sb[:], bank[:])
+            else:
+                nc.vector.tensor_copy(p_sb[:], bank[:])
+            ends = sb(f"ends{t}", [P, E], F32)
+            fetch(ends[:], p_sb, l6[:], so_sb[:, t : t + 1])
+            nc.vector.tensor_copy(pages[t][:].indirect(l7[:]), ends[:])
+            nc.sync.dma_start(out[t * P : (t + 1) * P, :], pages[t][:])

@@ -19,6 +19,7 @@ FLOPS = 2 * K * R * J + 2 * Z * R * J + 2 * R * N * O
 P = 128
 PACK = 4
 HALF = J // 2
+PART = O // 2
 QUADS = 4
 
 
@@ -31,8 +32,8 @@ def tile_picked_largercode_plain_bank_codedlevel_one_posted_kernel(
         keep = ctx.enter_context(tc.tile_pool(name="keep", bufs=1))
         psum = ctx.enter_context(tc.psum_pool(name="psum", bufs=1))
 
-        def sb(name, shape, dtype):
-            return keep.tile(shape, dtype, name=name, align_bytes=64)
+        def sb(name, shape, dtype, tag=None):
+            return keep.tile(shape, dtype, name=name, tag=tag or name, align_bytes=64)
 
         def load_list(name, src):
             lst = sb(name, list(src.shape), U16)
@@ -54,9 +55,9 @@ def tile_picked_largercode_plain_bank_codedlevel_one_posted_kernel(
             nc.sync.dma_start(words[:].bitcast(I32), src.bitcast(I32))
             return words
 
-        def stage_scales(stage, src, first):
+        def stage_scales(stage, src, first, queue):
             rows = src[0].bitcast(I32).rearrange("(q r) c -> r q c", r=4)
-            nc.sync.dma_start(stage[:, :, first : first + rows.shape[2]], rows)
+            queue.dma_start(stage[:, :, first : first + rows.shape[2]], rows)
 
         def spread_scales(plane, stage):
             words = plane[:].bitcast(I32)
@@ -65,57 +66,60 @@ def tile_picked_largercode_plain_bank_codedlevel_one_posted_kernel(
                 nc.vector.tensor_copy(words[32 * q : 32 * q + 4, :], stage[:, q, :])
 
         ga_sb = load_factor("ga_sb", ga, nc.scalar)
-        gb_sb = load_factor("gb_sb", gb, nc.scalar)
-        sl_sb = load_factor("sl_sb", sl, nc.gpsimd)
-        sa_sb = load_factor("sa_sb", sa, nc.gpsimd)
-        so_sb = sb("so_sb", [P, N // P], F32)
-        with nc.allow_non_contiguous_dma(reason="one factor a partition for each output tile"):
-            nc.gpsimd.dma_start(so_sb[:], so.rearrange("(t p) o -> p (t o)", p=P))
         xo_stage = sb("xo_stage", [4, QUADS, M // 4], I32)
-        w_stage = sb("w_stage", [4, QUADS, (R + R + N) // 4], I32)
+        w_stage = sb("w_stage", [4, QUADS, 2 * R // 4], I32)
+        wb_stage = sb("wb_stage", [4, QUADS, N // 4], I32)
+        stage_scales(w_stage, w2_scales, R // 4, nc.scalar)
+        stage_scales(w_stage, w_scales, 0, nc.scalar)
+        stage_scales(xo_stage, xo_scales, 0, nc.scalar)
 
         ta_sb, tb_sb, tl_sb = [], [], []
-        ta_sb.append(load_rows("ta0", ta, 0))
         l1 = load_list("l1", offs)
+        ta_sb.append(load_rows("ta0", ta, 0))
         tb_sb.append(load_rows("tb0", tb, 0))
         l2 = load_list("l2", offs2)
+        gb_sb = load_factor("gb_sb", gb, nc.sync)
         ta_sb.append(load_rows("ta1", ta, 1))
-        stage_scales(xo_stage, xo_scales, 0)
         tb_sb.append(load_rows("tb1", tb, 1))
         l3 = load_list("l3", offs3)
+        stage_scales(wb_stage, wb_scales, 0, nc.sync)
         xo_sb = load_words("xo_sb", xo_words[0].rearrange("p n t -> p (n t)"), U32, M)
-        stage_scales(w_stage, w2_scales, R // 4)
-        ta_sb.append(load_rows("ta2", ta, 2))
-        stage_scales(w_stage, w_scales, 0)
         w2_sb = load_words("w2_sb", w2_words[0], U8, 2 * R)
-        stage_scales(w_stage, wb_scales, 2 * R // 4)
+        ta_sb.append(load_rows("ta2", ta, 2))
         tb_sb.append(load_rows("tb2", tb, 2))
         w_sb = load_words("w_sb", w_words[0].rearrange("p n t -> p (n t)"), I32, R)
         ta_sb.append(load_rows("ta3", ta, 3))
         tb_sb.append(load_rows("tb3", tb, 3))
         l5 = load_list("l5", offs5)
+        sl_sb = load_factor("sl_sb", sl, nc.sync)
         tl_sb.append(load_rows("tl0", tl, 0))
-        l4 = load_list("l4", offs4)
         for t in range(1, PACK):
             tl_sb.append(load_rows(f"tl{t}", tl, t))
+        l4 = load_list("l4", offs4)
+        sa_sb = load_factor("sa_sb", sa, nc.sync)
         wb_sb = load_words("wb_sb", wb_words[0], U8, 2 * N)
         l6 = load_list("l6", offs6)
+        so_sb = sb("so_sb", [P, N // P], F32)
+        with nc.allow_non_contiguous_dma(reason="one factor a partition for each output tile"):
+            nc.sync.dma_start(so_sb[:], so.rearrange("(t p) o -> p (t o)", p=P))
         l7 = load_list("l7", offs7)
 
         pages = [sb(f"page{t}", [P, G], F32) for t in range(N // P)]
         for page in pages:
             nc.vector.memset(page[:], 0.0)
-        xo_plane = sb("xo_plane", [P, M], U8)
-        spread_scales(xo_plane, xo_stage)
-        w_plane = sb("w_plane", [P, R + R + N], U8)
+        w_plane = sb("w_plane", [P, 2 * R], U8)
         spread_scales(w_plane, w_stage)
         dealt_plane = sb("dealt_plane", [P, 2, R], U8)
         nc.vector.tensor_copy(
             dealt_plane[:].rearrange("p a (t m) -> p a t m", t=PACK),
-            w_plane[:, : 2 * R].rearrange("p (a m t) -> p a t m", a=2, t=PACK),
+            w_plane[:].rearrange("p (a m t) -> p a t m", a=2, t=PACK),
         )
+        xo_plane = sb("xo_plane", [P, M], U8)
+        spread_scales(xo_plane, xo_stage)
         xo_picked_scales = sb("xo_picked_scales", [P, J], U8)
         nc.vector.tensor_copy(xo_picked_scales[:], xo_plane[:].indirect(l3[:]))
+        wb_plane = sb("wb_plane", [P, N], U8)
+        spread_scales(wb_plane, wb_stage)
 
         def fetch(dst, window, offsets, factor):
             nc.scalar.activation(dst, window[:].indirect(offsets), COPY, scale=factor)
@@ -128,15 +132,11 @@ def tile_picked_largercode_plain_bank_codedlevel_one_posted_kernel(
                 MAX,
             )
 
-        xc = [sb(f"xc{h}", [P, HALF, PACK], BF16) for h in range(2)]
         low_a = sb("low_a", [P, 2, J], F32)
         low_b = sb("low_b", [P, 2, J], F32)
         for t in range(2):
             fetch(low_a[:, t, :], ta_sb[t], l1[:], ga_sb[:, t : t + 1])
             fetch(low_b[:, t, :], tb_sb[t], l2[:], gb_sb[:, t : t + 1])
-        for h in range(2):
-            cols = slice(h * HALF, (h + 1) * HALF)
-            larger_pair(xc[h], low_a[:, :, cols], low_b[:, :, cols], 0)
 
         xo_picked = sb("xo_picked", [P, J], U32)
         nc.vector.tensor_copy(xo_picked[:], xo_sb[:].indirect(l3[:]))
@@ -145,24 +145,27 @@ def tile_picked_largercode_plain_bank_codedlevel_one_posted_kernel(
             w2_dealt[:].rearrange("p (t m b) -> p t m b", t=PACK, b=2),
             w2_sb[:].rearrange("p (m t b) -> p t m b", t=PACK, b=2),
         )
-        w_dealt = sb("w_dealt", [P, R], I32)
+        w_dealt = sb("w_dealt", [P, R], I32, "wb_stage")
         nc.vector.tensor_copy(
             w_dealt[:].rearrange("p (t m) -> p t m", t=PACK),
             w_sb[:].rearrange("p (m t) -> p t m", t=PACK),
         )
-        banks = [[psum.tile([P, HALF], F32, name=f"bank{h}{t}") for t in range(PACK)] for h in range(2)]
+        banks = [psum.tile([P, J], F32, name=f"a_bank{t}") for t in range(PACK)]
+        for t in range(PACK):
+            nc.tensor.matmul_mx(
+                out=banks[t][:],
+                lhsT=w2_dealt[:, 2 * P * t : 2 * P * (t + 1)].bitcast(FP4X4),
+                lhsT_scale=dealt_plane[:, 1, P * t : P * (t + 1)],
+                rhs=xo_picked[:].bitcast(FP8X4),
+                rhs_scale=xo_picked_scales[:],
+                start=True,
+                stop=False,
+            )
+
+        xc = [sb(f"xc{h}", [P, HALF, PACK], BF16) for h in range(2)]
         for h in range(2):
             cols = slice(h * HALF, (h + 1) * HALF)
-            for t in range(PACK):
-                nc.tensor.matmul_mx(
-                    out=banks[h][t][:],
-                    lhsT=w2_dealt[:, 2 * P * t : 2 * P * (t + 1)].bitcast(FP4X4),
-                    lhsT_scale=dealt_plane[:, 1, P * t : P * (t + 1)],
-                    rhs=xo_picked[:, cols].bitcast(FP8X4),
-                    rhs_scale=xo_picked_scales[:, cols],
-                    start=True,
-                    stop=False,
-                )
+            larger_pair(xc[h], low_a[:, :, cols], low_b[:, :, cols], 0)
 
         high_a = [sb(f"high_a{h}", [P, 2, HALF], F32) for h in range(2)]
         high_b = [sb(f"high_b{h}", [P, 2, HALF], F32) for h in range(2)]
@@ -183,51 +186,63 @@ def tile_picked_largercode_plain_bank_codedlevel_one_posted_kernel(
             )
             for t in range(PACK):
                 nc.tensor.matmul_mx(
-                    out=banks[h][t][:],
+                    out=banks[t][:, h * HALF : (h + 1) * HALF],
                     lhsT=w_dealt[:, P * t : P * (t + 1)].bitcast(FP8X4),
                     lhsT_scale=dealt_plane[:, 0, P * t : P * (t + 1)],
                     rhs=xc_codes[h][:].bitcast(FP8X4),
                     rhs_scale=xc_scales[h][:],
                     start=False,
-                    stop=True,
+                    stop=(h == 1),
                 )
 
         a_sb = [sb(f"a{t}", [P, J], F32) for t in range(PACK)]
-        hid = sb("hid", [P, O, PACK], BF16)
-        hid_a = [sb(f"hid_a{u}", [P, 2, O], F32) for u in range(2)]
         hid_l = [sb(f"hid_l{u}", [P, 2, O], F32) for u in range(2)]
         for t in range(PACK):
-            for h in range(2):
-                nc.vector.tensor_copy(a_sb[t][:, h * HALF : (h + 1) * HALF], banks[h][t][:])
-        for t in range(PACK):
-            fetch(hid_a[t // 2][:, t % 2, :], a_sb[t], l4[:], sa_sb[:, t : t + 1])
             fetch(hid_l[t // 2][:, t % 2, :], tl_sb[t], l5[:], sl_sb[:, t : t + 1])
-            if t % 2 == 1:
-                larger_pair(hid, hid_a[t // 2][:], hid_l[t // 2][:], t // 2)
-        hid_codes = sb("hid_codes", [P, O], U32)
-        hid_scales = sb("hid_scales", [P, O], U8)
-        nc.vector.quantize_mx(
-            out=hid_codes[:].bitcast(FP8X4),
-            scales=hid_scales[:],
-            in_=hid[:].rearrange("p o t -> p (o t)"),
-        )
+        for t in range(PACK):
+            nc.vector.tensor_copy(a_sb[t][:], banks[t][:])
+        hid = [sb(f"hid{h}", [P, PART, PACK], BF16, f"xc_codes{h}") for h in range(2)]
+        low_h = sb("low_h", [P, 2, O], F32, "sl_sb")
+        for t in range(2):
+            fetch(low_h[:, t, :], a_sb[t], l4[:], sa_sb[:, t : t + 1])
+        for h in range(2):
+            cols = slice(h * PART, (h + 1) * PART)
+            larger_pair(hid[h], low_h[:, :, cols], hid_l[0][:, :, cols], 0)
+        high_h = [sb(f"high_h{h}", [P, 2, PART], F32) for h in range(2)]
+        for h in range(2):
+            entries = slice(h * PART // 16, (h + 1) * PART // 16)
+            for t in range(2, PACK):
+                fetch(high_h[h][:, t - 2, :], a_sb[t], l4[:, entries], sa_sb[:, t : t + 1])
+        hid_codes = [sb(f"hid_codes{h}", [P, PART], U32) for h in range(2)]
+        hid_scales = [sb(f"hid_scales{h}", [P, PART], U8) for h in range(2)]
+        p_banks = [psum.tile([P, O], F32, name=f"p_bank{t}") for t in range(N // P)]
+        for h in range(2):
+            cols = slice(h * PART, (h + 1) * PART)
+            larger_pair(hid[h], high_h[h][:], hid_l[1][:, :, cols], 1)
+        for h in range(2):
+            cols = slice(h * PART, (h + 1) * PART)
+            nc.vector.quantize_mx(
+                out=hid_codes[h][:].bitcast(FP8X4),
+                scales=hid_scales[h][:],
+                in_=hid[h][:].rearrange("p o t -> p (o t)"),
+            )
+            for t in range(N // P):
+                nc.tensor.matmul_mx(
+                    out=p_banks[t][:, cols],
+                    lhsT=wb_sb[:, 2 * P * t : 2 * P * (t + 1)].bitcast(FP4X4),
+                    lhsT_scale=wb_plane[:, P * t : P * (t + 1)],
+                    rhs=hid_codes[h][:].bitcast(FP8X4),
+                    rhs_scale=hid_scales[h][:],
+                    start=True,
+                    stop=True,
+                )
 
         for t in range(N // P):
-            bank = psum.tile([P, O], F32, name=f"bank0{t}")
-            nc.tensor.matmul_mx(
-                out=bank[:],
-                lhsT=wb_sb[:, 2 * P * t : 2 * P * (t + 1)].bitcast(FP4X4),
-                lhsT_scale=w_plane[:, 2 * R + P * t : 2 * R + P * (t + 1)],
-                rhs=hid_codes[:].bitcast(FP8X4),
-                rhs_scale=hid_scales[:],
-                start=True,
-                stop=True,
-            )
             p_sb = sb(f"p{t}", [P, O], F32)
             if t == 0:
-                nc.scalar.copy(p_sb[:], bank[:])
+                nc.scalar.copy(p_sb[:], p_banks[t][:])
             else:
-                nc.vector.tensor_copy(p_sb[:], bank[:])
+                nc.vector.tensor_copy(p_sb[:], p_banks[t][:])
             ends = sb(f"ends{t}", [P, E], F32)
             fetch(ends[:], p_sb, l6[:], so_sb[:, t : t + 1])
             nc.vector.tensor_copy(pages[t][:].indirect(l7[:]), ends[:])

@@ -65,6 +65,9 @@ def tile_picked_largercode_plain_bank_codedlevel_one_posted_kernel(
             for q in range(QUADS):
                 nc.vector.tensor_copy(words[32 * q : 32 * q + 4, :], stage[:, q, :])
 
+        idle = sb("idle", [P, 2], F32)
+        nc.vector.memset(idle[:, 0:1], 0.0)
+        nc.scalar.activation(idle[:, 1:2], idle[:, 0:1], COPY)
         ga_sb = load_factor("ga_sb", ga, nc.scalar)
         xo_stage = sb("xo_stage", [4, QUADS, M // 4], I32)
         w_stage = sb("w_stage", [4, QUADS, 2 * R // 4], I32)

@@ -13,14 +13,17 @@ FP4X4 = mybir.dt.float4_e2m1fn_x4
 COPY = mybir.ActivationFunctionType.Copy
 MAX = mybir.AluOpType.max
 
-K, J, R, T, Z, M, O, D, N, E, G = 512, 512, 512, 1024, 512, 1024, 256, 1024, 256, 128, 512
+K, J, R, Z, M, O, N, E, G = 512, 512, 512, 512, 1024, 256, 256, 128, 512
 FLOPS = 2 * K * R * J + 2 * Z * R * J + 2 * R * N * O
 
 P = 128
 PACK = 4
-HALF = J // 2
-PART = O // 2
-QUADS = 4
+QUADRANTS = 4
+SCALE_ROWS = 4
+LIST_ROWS = 16
+J_HALF = J // 2
+O_HALF = O // 2
+N_TILES = N // P
 
 
 def tile_picked_largercode_plain_bank_codedlevel_one_posted_kernel(
@@ -36,9 +39,9 @@ def tile_picked_largercode_plain_bank_codedlevel_one_posted_kernel(
             return keep.tile(shape, dtype, name=name, tag=tag or name, align_bytes=64)
 
         def load_list(name, src):
-            lst = sb(name, list(src.shape), U16)
-            nc.sync.dma_start(lst[:], src)
-            return lst
+            offsets = sb(name, list(src.shape), U16)
+            nc.sync.dma_start(offsets[:], src)
+            return offsets
 
         def load_rows(name, src, t):
             rows = sb(name, [P, src.shape[1]], F32)
@@ -46,37 +49,52 @@ def tile_picked_largercode_plain_bank_codedlevel_one_posted_kernel(
             return rows
 
         def load_factor(name, src, queue):
-            fac = sb(name, [P, PACK], F32)
-            queue.dma_start(fac[:], src.rearrange("(p t) o -> p (t o)", t=PACK))
-            return fac
+            factor = sb(name, [P, PACK], F32)
+            queue.dma_start(factor[:], src.rearrange("(p t) o -> p (t o)", t=PACK))
+            return factor
 
         def load_words(name, src, dtype, cols):
             words = sb(name, [P, cols], dtype)
             nc.sync.dma_start(words[:].bitcast(I32), src.bitcast(I32))
             return words
 
-        def stage_scales(stage, src, first, queue):
-            rows = src[0].bitcast(I32).rearrange("(q r) c -> r q c", r=4)
-            queue.dma_start(stage[:, :, first : first + rows.shape[2]], rows)
+        def stage_scales(stage, src, first):
+            rows = src[0].bitcast(I32).rearrange("(q r) c -> r q c", r=SCALE_ROWS)
+            nc.scalar.dma_start(stage[:, :, first : first + rows.shape[2]], rows)
 
         def spread_scales(plane, stage):
             words = plane[:].bitcast(I32)
             nc.vector.memset(words, 0)
-            for q in range(QUADS):
-                nc.vector.tensor_copy(words[32 * q : 32 * q + 4, :], stage[:, q, :])
+            for q in range(QUADRANTS):
+                nc.vector.tensor_copy(words[32 * q : 32 * q + SCALE_ROWS, :], stage[:, q, :])
 
-        idle = sb("idle", [P, 2], F32)
-        nc.vector.memset(idle[:, 0:1], 0.0)
-        nc.scalar.activation(idle[:, 1:2], idle[:, 0:1], COPY)
+        def fetch(dst, window, offsets, factor):
+            nc.scalar.activation(dst, window[:].indirect(offsets), COPY, scale=factor)
+
+        def larger_pair(dst, first, second, u):
+            nc.vector.tensor_tensor(
+                dst[:, :, 2 * u : 2 * u + 2],
+                first.rearrange("p t c -> p c t"),
+                second.rearrange("p t c -> p c t"),
+                MAX,
+            )
+
+        def quantise(codes, scales, values):
+            nc.vector.quantize_mx(
+                out=codes[:].bitcast(FP8X4), scales=scales[:], in_=values[:].rearrange("p c t -> p (c t)")
+            )
+
+        def half(h, width):
+            return slice(h * width, (h + 1) * width)
+
         ga_sb = load_factor("ga_sb", ga, nc.scalar)
-        xo_stage = sb("xo_stage", [4, QUADS, M // 4], I32)
-        w_stage = sb("w_stage", [4, QUADS, 2 * R // 4], I32)
-        wb_stage = sb("wb_stage", [4, QUADS, N // 4], I32)
-        stage_scales(w_stage, w2_scales, R // 4, nc.scalar)
-        stage_scales(w_stage, w_scales, 0, nc.scalar)
-        stage_scales(xo_stage, xo_scales, 0, nc.scalar)
+        xo_stage = sb("xo_stage", [SCALE_ROWS, QUADRANTS, M // 4], I32)
+        w_stage = sb("w_stage", [SCALE_ROWS, QUADRANTS, 2 * R // 4], I32)
+        stage_scales(w_stage, w2_scales, R // 4)
+        stage_scales(w_stage, w_scales, 0)
+        stage_scales(xo_stage, xo_scales, 0)
 
-        ta_sb, tb_sb, tl_sb = [], [], []
+        ta_sb, tb_sb = [], []
         l1 = load_list("l1", offs)
         ta_sb.append(load_rows("ta0", ta, 0))
         tb_sb.append(load_rows("tb0", tb, 0))
@@ -85,31 +103,35 @@ def tile_picked_largercode_plain_bank_codedlevel_one_posted_kernel(
         ta_sb.append(load_rows("ta1", ta, 1))
         tb_sb.append(load_rows("tb1", tb, 1))
         l3 = load_list("l3", offs3)
-        stage_scales(wb_stage, wb_scales, 0, nc.sync)
         xo_sb = load_words("xo_sb", xo_words[0].rearrange("p n t -> p (n t)"), U32, M)
         w2_sb = load_words("w2_sb", w2_words[0], U8, 2 * R)
-        ta_sb.append(load_rows("ta2", ta, 2))
-        tb_sb.append(load_rows("tb2", tb, 2))
+        for t in range(2, PACK):
+            ta_sb.append(load_rows(f"ta{t}", ta, t))
+            tb_sb.append(load_rows(f"tb{t}", tb, t))
         w_sb = load_words("w_sb", w_words[0].rearrange("p n t -> p (n t)"), I32, R)
-        ta_sb.append(load_rows("ta3", ta, 3))
-        tb_sb.append(load_rows("tb3", tb, 3))
         l5 = load_list("l5", offs5)
         sl_sb = load_factor("sl_sb", sl, nc.sync)
-        tl_sb.append(load_rows("tl0", tl, 0))
-        for t in range(1, PACK):
-            tl_sb.append(load_rows(f"tl{t}", tl, t))
+        tl_sb = [load_rows(f"tl{t}", tl, t) for t in range(PACK)]
         l4 = load_list("l4", offs4)
         sa_sb = load_factor("sa_sb", sa, nc.sync)
         wb_sb = load_words("wb_sb", wb_words[0], U8, 2 * N)
+        wb_plane = sb("wb_plane", [P, N], U8)
+        nc.vector.memset(wb_plane[:].bitcast(I32), 0)
+        for q in range(QUADRANTS):
+            nc.sync.dma_start(
+                wb_plane[:].bitcast(I32)[32 * q : 32 * q + SCALE_ROWS, :],
+                wb_scales[0].bitcast(I32)[SCALE_ROWS * q : SCALE_ROWS * (q + 1), :],
+            )
         l6 = load_list("l6", offs6)
-        so_sb = sb("so_sb", [P, N // P], F32)
+        so_sb = sb("so_sb", [P, N_TILES], F32)
         with nc.allow_non_contiguous_dma(reason="one factor a partition for each output tile"):
             nc.sync.dma_start(so_sb[:], so.rearrange("(t p) o -> p (t o)", p=P))
         l7 = load_list("l7", offs7)
 
-        pages = [sb(f"page{t}", [P, G], F32) for t in range(N // P)]
+        pages = [sb(f"page{t}", [P, G], F32) for t in range(N_TILES)]
         for page in pages:
             nc.vector.memset(page[:], 0.0)
+
         w_plane = sb("w_plane", [P, 2 * R], U8)
         spread_scales(w_plane, w_stage)
         dealt_plane = sb("dealt_plane", [P, 2, R], U8)
@@ -121,42 +143,35 @@ def tile_picked_largercode_plain_bank_codedlevel_one_posted_kernel(
         spread_scales(xo_plane, xo_stage)
         xo_picked_scales = sb("xo_picked_scales", [P, J], U8)
         nc.vector.tensor_copy(xo_picked_scales[:], xo_plane[:].indirect(l3[:]))
-        wb_plane = sb("wb_plane", [P, N], U8)
-        spread_scales(wb_plane, wb_stage)
-
-        def fetch(dst, window, offsets, factor):
-            nc.scalar.activation(dst, window[:].indirect(offsets), COPY, scale=factor)
-
-        def larger_pair(dst, first, second, u):
-            nc.vector.tensor_tensor(
-                dst[:, :, 2 * u : 2 * u + 2],
-                first.rearrange("p t j -> p j t"),
-                second.rearrange("p t j -> p j t"),
-                MAX,
-            )
 
         low_a = sb("low_a", [P, 2, J], F32)
         low_b = sb("low_b", [P, 2, J], F32)
         for t in range(2):
             fetch(low_a[:, t, :], ta_sb[t], l1[:], ga_sb[:, t : t + 1])
             fetch(low_b[:, t, :], tb_sb[t], l2[:], gb_sb[:, t : t + 1])
+        high_a = [sb(f"high_a{h}", [P, 2, J_HALF], F32) for h in range(2)]
+        high_b = [sb(f"high_b{h}", [P, 2, J_HALF], F32) for h in range(2)]
+        for t in range(2, PACK):
+            for h in range(2):
+                entries = half(h, J_HALF // LIST_ROWS)
+                fetch(high_a[h][:, t - 2, :], ta_sb[t], l1[:, entries], ga_sb[:, t : t + 1])
+                fetch(high_b[h][:, t - 2, :], tb_sb[t], l2[:, entries], gb_sb[:, t : t + 1])
+        xc = [sb(f"xc{h}", [P, J_HALF, PACK], BF16) for h in range(2)]
+        for h in range(2):
+            cols = half(h, J_HALF)
+            larger_pair(xc[h], low_a[:, :, cols], low_b[:, :, cols], 0)
 
         xo_picked = sb("xo_picked", [P, J], U32)
         nc.vector.tensor_copy(xo_picked[:], xo_sb[:].indirect(l3[:]))
-        w2_dealt = sb("w2_dealt", [P, 2 * R], U8)
+        w2_dealt = sb("w2_dealt", [P, 2 * R], U8, "tb2")
         nc.vector.tensor_copy(
             w2_dealt[:].rearrange("p (t m b) -> p t m b", t=PACK, b=2),
             w2_sb[:].rearrange("p (m t b) -> p t m b", t=PACK, b=2),
         )
-        w_dealt = sb("w_dealt", [P, R], I32, "wb_stage")
-        nc.vector.tensor_copy(
-            w_dealt[:].rearrange("p (t m) -> p t m", t=PACK),
-            w_sb[:].rearrange("p (m t) -> p t m", t=PACK),
-        )
-        banks = [psum.tile([P, J], F32, name=f"a_bank{t}") for t in range(PACK)]
+        a_banks = [psum.tile([P, J], F32, name=f"a_bank{t}") for t in range(PACK)]
         for t in range(PACK):
             nc.tensor.matmul_mx(
-                out=banks[t][:],
+                out=a_banks[t][:],
                 lhsT=w2_dealt[:, 2 * P * t : 2 * P * (t + 1)].bitcast(FP4X4),
                 lhsT_scale=dealt_plane[:, 1, P * t : P * (t + 1)],
                 rhs=xo_picked[:].bitcast(FP8X4),
@@ -165,31 +180,20 @@ def tile_picked_largercode_plain_bank_codedlevel_one_posted_kernel(
                 stop=False,
             )
 
-        xc = [sb(f"xc{h}", [P, HALF, PACK], BF16) for h in range(2)]
-        for h in range(2):
-            cols = slice(h * HALF, (h + 1) * HALF)
-            larger_pair(xc[h], low_a[:, :, cols], low_b[:, :, cols], 0)
-
-        high_a = [sb(f"high_a{h}", [P, 2, HALF], F32) for h in range(2)]
-        high_b = [sb(f"high_b{h}", [P, 2, HALF], F32) for h in range(2)]
-        for t in range(2, PACK):
-            for h in range(2):
-                entries = slice(h * HALF // 16, (h + 1) * HALF // 16)
-                fetch(high_a[h][:, t - 2, :], ta_sb[t], l1[:, entries], ga_sb[:, t : t + 1])
-                fetch(high_b[h][:, t - 2, :], tb_sb[t], l2[:, entries], gb_sb[:, t : t + 1])
-        xc_codes = [sb(f"xc_codes{h}", [P, HALF], U32) for h in range(2)]
-        xc_scales = [sb(f"xc_scales{h}", [P, HALF], U8) for h in range(2)]
+        w_dealt = sb("w_dealt", [P, R], I32)
+        nc.vector.tensor_copy(
+            w_dealt[:].rearrange("p (t m) -> p t m", t=PACK),
+            w_sb[:].rearrange("p (m t) -> p t m", t=PACK),
+        )
+        xc_codes = [sb(f"xc_codes{h}", [P, J_HALF], U32) for h in range(2)]
+        xc_scales = [sb(f"xc_scales{h}", [P, J_HALF], U8) for h in range(2)]
         for h in range(2):
             larger_pair(xc[h], high_a[h][:], high_b[h][:], 1)
         for h in range(2):
-            nc.vector.quantize_mx(
-                out=xc_codes[h][:].bitcast(FP8X4),
-                scales=xc_scales[h][:],
-                in_=xc[h][:].rearrange("p j t -> p (j t)"),
-            )
+            quantise(xc_codes[h], xc_scales[h], xc[h])
             for t in range(PACK):
                 nc.tensor.matmul_mx(
-                    out=banks[t][:, h * HALF : (h + 1) * HALF],
+                    out=a_banks[t][:, half(h, J_HALF)],
                     lhsT=w_dealt[:, P * t : P * (t + 1)].bitcast(FP8X4),
                     lhsT_scale=dealt_plane[:, 0, P * t : P * (t + 1)],
                     rhs=xc_codes[h][:].bitcast(FP8X4),
@@ -198,40 +202,35 @@ def tile_picked_largercode_plain_bank_codedlevel_one_posted_kernel(
                     stop=(h == 1),
                 )
 
+        levels = [sb(f"levels{u}", [P, 2, O], F32) for u in range(2)]
+        for t in range(PACK):
+            fetch(levels[t // 2][:, t % 2, :], tl_sb[t], l5[:], sl_sb[:, t : t + 1])
         a_sb = [sb(f"a{t}", [P, J], F32) for t in range(PACK)]
-        hid_l = [sb(f"hid_l{u}", [P, 2, O], F32) for u in range(2)]
         for t in range(PACK):
-            fetch(hid_l[t // 2][:, t % 2, :], tl_sb[t], l5[:], sl_sb[:, t : t + 1])
-        for t in range(PACK):
-            nc.vector.tensor_copy(a_sb[t][:], banks[t][:])
-        hid = [sb(f"hid{h}", [P, PART, PACK], BF16, f"xc_codes{h}") for h in range(2)]
-        low_h = sb("low_h", [P, 2, O], F32, "sl_sb")
+            nc.vector.tensor_copy(a_sb[t][:], a_banks[t][:])
+        hid = [sb(f"hid{h}", [P, O_HALF, PACK], BF16, f"xc_codes{h}") for h in range(2)]
+        low_h = sb("low_h", [P, 2, O], F32, "tl2")
         for t in range(2):
             fetch(low_h[:, t, :], a_sb[t], l4[:], sa_sb[:, t : t + 1])
         for h in range(2):
-            cols = slice(h * PART, (h + 1) * PART)
-            larger_pair(hid[h], low_h[:, :, cols], hid_l[0][:, :, cols], 0)
-        high_h = [sb(f"high_h{h}", [P, 2, PART], F32) for h in range(2)]
+            cols = half(h, O_HALF)
+            larger_pair(hid[h], low_h[:, :, cols], levels[0][:, :, cols], 0)
+        high_h = [sb("high_h0", [P, 2, O_HALF], F32, "tl3"), sb("high_h1", [P, 2, O_HALF], F32)]
         for h in range(2):
-            entries = slice(h * PART // 16, (h + 1) * PART // 16)
+            entries = half(h, O_HALF // LIST_ROWS)
             for t in range(2, PACK):
                 fetch(high_h[h][:, t - 2, :], a_sb[t], l4[:, entries], sa_sb[:, t : t + 1])
-        hid_codes = [sb(f"hid_codes{h}", [P, PART], U32) for h in range(2)]
-        hid_scales = [sb(f"hid_scales{h}", [P, PART], U8) for h in range(2)]
-        p_banks = [psum.tile([P, O], F32, name=f"p_bank{t}") for t in range(N // P)]
         for h in range(2):
-            cols = slice(h * PART, (h + 1) * PART)
-            larger_pair(hid[h], high_h[h][:], hid_l[1][:, :, cols], 1)
+            larger_pair(hid[h], high_h[h][:], levels[1][:, :, half(h, O_HALF)], 1)
+
+        hid_codes = [sb(f"hid_codes{h}", [P, O_HALF], U32) for h in range(2)]
+        hid_scales = [sb(f"hid_scales{h}", [P, O_HALF], U8) for h in range(2)]
+        p_banks = [[psum.tile([P, O_HALF], F32, name=f"p_bank{t}{h}") for h in range(2)] for t in range(N_TILES)]
         for h in range(2):
-            cols = slice(h * PART, (h + 1) * PART)
-            nc.vector.quantize_mx(
-                out=hid_codes[h][:].bitcast(FP8X4),
-                scales=hid_scales[h][:],
-                in_=hid[h][:].rearrange("p o t -> p (o t)"),
-            )
-            for t in range(N // P):
+            quantise(hid_codes[h], hid_scales[h], hid[h])
+            for t in range(N_TILES):
                 nc.tensor.matmul_mx(
-                    out=p_banks[t][:, cols],
+                    out=p_banks[t][h][:],
                     lhsT=wb_sb[:, 2 * P * t : 2 * P * (t + 1)].bitcast(FP4X4),
                     lhsT_scale=wb_plane[:, P * t : P * (t + 1)],
                     rhs=hid_codes[h][:].bitcast(FP8X4),
@@ -240,12 +239,11 @@ def tile_picked_largercode_plain_bank_codedlevel_one_posted_kernel(
                     stop=True,
                 )
 
-        for t in range(N // P):
+        empty_bank = (nc.scalar.copy, nc.vector.tensor_copy)
+        for t in range(N_TILES):
             p_sb = sb(f"p{t}", [P, O], F32)
-            if t == 0:
-                nc.scalar.copy(p_sb[:], p_banks[t][:])
-            else:
-                nc.vector.tensor_copy(p_sb[:], p_banks[t][:])
+            for h in range(2):
+                empty_bank[t](p_sb[:, half(h, O_HALF)], p_banks[t][h][:])
             ends = sb(f"ends{t}", [P, E], F32)
             fetch(ends[:], p_sb, l6[:], so_sb[:, t : t + 1])
             nc.vector.tensor_copy(pages[t][:].indirect(l7[:]), ends[:])

from contextlib import ExitStack

import concourse.mybir as mybir

F32 = mybir.dt.float32
BF16 = mybir.dt.bfloat16
I32 = mybir.dt.int32
U32 = mybir.dt.uint32
U16 = mybir.dt.uint16
U8 = mybir.dt.uint8
FP8X4 = mybir.dt.float8_e4m3fn_x4
FP4X4 = mybir.dt.float4_e2m1fn_x4
COPY = mybir.ActivationFunctionType.Copy
MAX = mybir.AluOpType.max

K, J, R, Z, M, O, N, E, G = 512, 512, 512, 512, 1024, 256, 256, 128, 512
FLOPS = 2 * K * R * J + 2 * Z * R * J + 2 * R * N * O

P = 128
PACK = 4
QUADRANTS = 4
SCALE_ROWS = 4
LIST_ROWS = 16
J_HALF = J // 2
O_HALF = O // 2
N_TILES = N // P


def tile_picked_largercode_plain_bank_codedlevel_one_posted_kernel(
    tc, ta, tb, ga, gb, w_words, w_scales, xo_words, xo_scales, w2_words, w2_scales, tl, sa, sl,
    wb_words, wb_scales, so, offs, offs2, offs3, offs4, offs5, offs6, offs7, out,
):
    nc = tc.nc
    with ExitStack() as ctx:
        keep = ctx.enter_context(tc.tile_pool(name="keep", bufs=1))
        psum = ctx.enter_context(tc.psum_pool(name="psum", bufs=1))

        def sb(name, shape, dtype, tag=None):
            return keep.tile(shape, dtype, name=name, tag=tag or name, align_bytes=64)

        def load_list(name, src):
            offsets = sb(name, list(src.shape), U16)
            nc.sync.dma_start(offsets[:], src)
            return offsets

        def load_rows(name, src, t):
            rows = sb(name, [P, src.shape[1]], F32)
            nc.sync.dma_start(rows[:], src.rearrange("(p t) c -> p t c", t=PACK)[:, t, :])
            return rows

        def load_factor(name, src, queue):
            factor = sb(name, [P, PACK], F32)
            queue.dma_start(factor[:], src.rearrange("(p t) o -> p (t o)", t=PACK))
            return factor

        def load_words(name, src, dtype, cols):
            words = sb(name, [P, cols], dtype)
            nc.sync.dma_start(words[:].bitcast(I32), src.bitcast(I32))
            return words

        def stage_scales(stage, src, first):
            rows = src[0].bitcast(I32).rearrange("(q r) c -> r q c", r=SCALE_ROWS)
            nc.scalar.dma_start(stage[:, :, first : first + rows.shape[2]], rows)

        def spread_scales(plane, stage):
            words = plane[:].bitcast(I32)
            nc.vector.memset(words, 0)
            for q in range(QUADRANTS):
                nc.vector.tensor_copy(words[32 * q : 32 * q + SCALE_ROWS, :], stage[:, q, :])

        def fetch(dst, window, offsets, factor):
            nc.scalar.activation(dst, window[:].indirect(offsets), COPY, scale=factor)

        def larger_pair(dst, first, second, u):
            nc.vector.tensor_tensor(
                dst[:, :, 2 * u : 2 * u + 2],
                first.rearrange("p t c -> p c t"),
                second.rearrange("p t c -> p c t"),
                MAX,
            )

        def quantise(codes, scales, values):
            nc.vector.quantize_mx(
                out=codes[:].bitcast(FP8X4), scales=scales[:], in_=values[:].rearrange("p c t -> p (c t)")
            )

        def half(h, width):
            return slice(h * width, (h + 1) * width)

        ga_sb = load_factor("ga_sb", ga, nc.scalar)
        xo_stage = sb("xo_stage", [SCALE_ROWS, QUADRANTS, M // 4], I32)
        w_stage = sb("w_stage", [SCALE_ROWS, QUADRANTS, 2 * R // 4], I32)
        stage_scales(w_stage, w2_scales, R // 4)
        stage_scales(w_stage, w_scales, 0)
        stage_scales(xo_stage, xo_scales, 0)

        ta_sb, tb_sb = [], []
        l1 = load_list("l1", offs)
        ta_sb.append(load_rows("ta0", ta, 0))
        tb_sb.append(load_rows("tb0", tb, 0))
        l2 = load_list("l2", offs2)
        gb_sb = load_factor("gb_sb", gb, nc.sync)
        ta_sb.append(load_rows("ta1", ta, 1))
        tb_sb.append(load_rows("tb1", tb, 1))
        l3 = load_list("l3", offs3)
        xo_sb = load_words("xo_sb", xo_words[0].rearrange("p n t -> p (n t)"), U32, M)
        w2_sb = load_words("w2_sb", w2_words[0], U8, 2 * R)
        for t in range(2, PACK):
            ta_sb.append(load_rows(f"ta{t}", ta, t))
            tb_sb.append(load_rows(f"tb{t}", tb, t))
        w_sb = load_words("w_sb", w_words[0].rearrange("p n t -> p (n t)"), I32, R)
        l5 = load_list("l5", offs5)
        sl_sb = load_factor("sl_sb", sl, nc.sync)
        tl_sb = [load_rows(f"tl{t}", tl, t) for t in range(PACK)]
        l4 = load_list("l4", offs4)
        sa_sb = load_factor("sa_sb", sa, nc.sync)
        wb_sb = load_words("wb_sb", wb_words[0], U8, 2 * N)
        wb_plane = sb("wb_plane", [P, N], U8)
        nc.vector.memset(wb_plane[:].bitcast(I32), 0)
        for q in range(QUADRANTS):
            nc.sync.dma_start(
                wb_plane[:].bitcast(I32)[32 * q : 32 * q + SCALE_ROWS, :],
                wb_scales[0].bitcast(I32)[SCALE_ROWS * q : SCALE_ROWS * (q + 1), :],
            )
        l6 = load_list("l6", offs6)
        so_sb = sb("so_sb", [P, N_TILES], F32)
        with nc.allow_non_contiguous_dma(reason="one factor a partition for each output tile"):
            nc.sync.dma_start(so_sb[:], so.rearrange("(t p) o -> p (t o)", p=P))
        l7 = load_list("l7", offs7)

        pages = [sb(f"page{t}", [P, G], F32) for t in range(N_TILES)]
        for page in pages:
            nc.vector.memset(page[:], 0.0)

        w_plane = sb("w_plane", [P, 2 * R], U8)
        spread_scales(w_plane, w_stage)
        dealt_plane = sb("dealt_plane", [P, 2, R], U8)
        nc.vector.tensor_copy(
            dealt_plane[:].rearrange("p a (t m) -> p a t m", t=PACK),
            w_plane[:].rearrange("p (a m t) -> p a t m", a=2, t=PACK),
        )
        xo_plane = sb("xo_plane", [P, M], U8)
        spread_scales(xo_plane, xo_stage)
        xo_picked_scales = sb("xo_picked_scales", [P, J], U8)
        nc.vector.tensor_copy(xo_picked_scales[:], xo_plane[:].indirect(l3[:]))

        low_a = sb("low_a", [P, 2, J], F32)
        low_b = sb("low_b", [P, 2, J], F32)
        for t in range(2):
            fetch(low_a[:, t, :], ta_sb[t], l1[:], ga_sb[:, t : t + 1])
            fetch(low_b[:, t, :], tb_sb[t], l2[:], gb_sb[:, t : t + 1])
        high_a = [sb(f"high_a{h}", [P, 2, J_HALF], F32) for h in range(2)]
        high_b = [sb(f"high_b{h}", [P, 2, J_HALF], F32) for h in range(2)]
        for t in range(2, PACK):
            for h in range(2):
                entries = half(h, J_HALF // LIST_ROWS)
                fetch(high_a[h][:, t - 2, :], ta_sb[t], l1[:, entries], ga_sb[:, t : t + 1])
                fetch(high_b[h][:, t - 2, :], tb_sb[t], l2[:, entries], gb_sb[:, t : t + 1])
        xc = [sb(f"xc{h}", [P, J_HALF, PACK], BF16) for h in range(2)]
        for h in range(2):
            cols = half(h, J_HALF)
            larger_pair(xc[h], low_a[:, :, cols], low_b[:, :, cols], 0)

        xo_picked = sb("xo_picked", [P, J], U32)
        nc.vector.tensor_copy(xo_picked[:], xo_sb[:].indirect(l3[:]))
        w2_dealt = sb("w2_dealt", [P, 2 * R], U8, "tb2")
        nc.vector.tensor_copy(
            w2_dealt[:].rearrange("p (t m b) -> p t m b", t=PACK, b=2),
            w2_sb[:].rearrange("p (m t b) -> p t m b", t=PACK, b=2),
        )
        a_banks = [psum.tile([P, J], F32, name=f"a_bank{t}") for t in range(PACK)]
        for t in range(PACK):
            nc.tensor.matmul_mx(
                out=a_banks[t][:],
                lhsT=w2_dealt[:, 2 * P * t : 2 * P * (t + 1)].bitcast(FP4X4),
                lhsT_scale=dealt_plane[:, 1, P * t : P * (t + 1)],
                rhs=xo_picked[:].bitcast(FP8X4),
                rhs_scale=xo_picked_scales[:],
                start=True,
                stop=False,
            )

        w_dealt = sb("w_dealt", [P, R], I32)
        nc.vector.tensor_copy(
            w_dealt[:].rearrange("p (t m) -> p t m", t=PACK),
            w_sb[:].rearrange("p (m t) -> p t m", t=PACK),
        )
        xc_codes = [sb(f"xc_codes{h}", [P, J_HALF], U32) for h in range(2)]
        xc_scales = [sb(f"xc_scales{h}", [P, J_HALF], U8) for h in range(2)]
        for h in range(2):
            larger_pair(xc[h], high_a[h][:], high_b[h][:], 1)
        for h in range(2):
            quantise(xc_codes[h], xc_scales[h], xc[h])
            for t in range(PACK):
                nc.tensor.matmul_mx(
                    out=a_banks[t][:, half(h, J_HALF)],
                    lhsT=w_dealt[:, P * t : P * (t + 1)].bitcast(FP8X4),
                    lhsT_scale=dealt_plane[:, 0, P * t : P * (t + 1)],
                    rhs=xc_codes[h][:].bitcast(FP8X4),
                    rhs_scale=xc_scales[h][:],
                    start=False,
                    stop=(h == 1),
                )

        levels = [sb(f"levels{u}", [P, 2, O], F32) for u in range(2)]
        for t in range(PACK):
            fetch(levels[t // 2][:, t % 2, :], tl_sb[t], l5[:], sl_sb[:, t : t + 1])
        a_sb = [sb(f"a{t}", [P, J], F32) for t in range(PACK)]
        for t in range(PACK):
            nc.vector.tensor_copy(a_sb[t][:], a_banks[t][:])
        hid = [sb(f"hid{h}", [P, O_HALF, PACK], BF16, f"xc_codes{h}") for h in range(2)]
        low_h = sb("low_h", [P, 2, O], F32, "tl2")
        for t in range(2):
            fetch(low_h[:, t, :], a_sb[t], l4[:], sa_sb[:, t : t + 1])
        for h in range(2):
            cols = half(h, O_HALF)
            larger_pair(hid[h], low_h[:, :, cols], levels[0][:, :, cols], 0)
        high_h = [sb("high_h0", [P, 2, O_HALF], F32, "tl3"), sb("high_h1", [P, 2, O_HALF], F32)]
        for h in range(2):
            entries = half(h, O_HALF // LIST_ROWS)
            for t in range(2, PACK):
                fetch(high_h[h][:, t - 2, :], a_sb[t], l4[:, entries], sa_sb[:, t : t + 1])
        for h in range(2):
            larger_pair(hid[h], high_h[h][:], levels[1][:, :, half(h, O_HALF)], 1)

        hid_codes = [sb(f"hid_codes{h}", [P, O_HALF], U32) for h in range(2)]
        hid_scales = [sb(f"hid_scales{h}", [P, O_HALF], U8) for h in range(2)]
        p_banks = [[psum.tile([P, O_HALF], F32, name=f"p_bank{t}{h}") for h in range(2)] for t in range(N_TILES)]
        for h in range(2):
            quantise(hid_codes[h], hid_scales[h], hid[h])
            for t in range(N_TILES):
                nc.tensor.matmul_mx(
                    out=p_banks[t][h][:],
                    lhsT=wb_sb[:, 2 * P * t : 2 * P * (t + 1)].bitcast(FP4X4),
                    lhsT_scale=wb_plane[:, P * t : P * (t + 1)],
                    rhs=hid_codes[h][:].bitcast(FP8X4),
                    rhs_scale=hid_scales[h][:],
                    start=True,
                    stop=True,
                )

        empty_bank = (nc.scalar.copy, nc.vector.tensor_copy)
        for t in range(N_TILES):
            p_sb = sb(f"p{t}", [P, O], F32)
            for h in range(2):
                empty_bank[t](p_sb[:, half(h, O_HALF)], p_banks[t][h][:])
            ends = sb(f"ends{t}", [P, E], F32)
            fetch(ends[:], p_sb, l6[:], so_sb[:, t : t + 1])
            nc.vector.tensor_copy(pages[t][:].indirect(l7[:]), ends[:])
            nc.sync.dma_start(out[t * P : (t + 1) * P, :], pages[t][:])
